import numpy as np
CORES = [64,68,72,76,80,84,88,92,96,100,104,108,112,116,120,124]
N = 16
def setup_inputs(rng):
    return {"x": rng.standard_normal((N, 128, 128), dtype=np.float32)}
def reference(x):
    b = 128 // N
    blocks = x.reshape(N, 128, N, b)
    return {"y": np.ascontiguousarray(blocks.transpose(2, 1, 0, 3)).reshape(N, 128, 128)}

from concourse.bass import DstId, RemoteDMATransfer

B = 8

SCRATCH = {
    "xs": ("sbuf", [128, 128], "float32"),
    "land": ("sbuf", [128, 128], "float32"),
    "relay": ("sbuf", [128, 32], "float32"),
}
SEMAPHORES = ["loaded", "own", "fed", "sent", "arrived", "stored"]


def engines(first, n):
    return ((1 << n) - 1) << first


def other_parity_chips(ch):
    return [8 + ((ch ^ 1) - 8 + 2 * i) % 8 for i in range(4)]


def same_parity_chips(ch):
    return [8 + (ch - 8 + 2 * i) % 8 for i in (1, 2, 3)]


def rank_program(g, core, T, topo):
    def to(dst, mask, sem, src, out):
        rid, pid, _se = topo.addr(dst)
        return RemoteDMATransfer(dst_ids=[DstId(rid=rid, pnc=pid)], dma_engine_mask=mask, remote_sem=sem,
                                 src=src, dst=out)

    ch, k = topo.chip(core), core % 8
    if ch < 8:
        return
    S = T.sem

    if k in (0, 4):
        r = T.rank_of(core)
        mine = slice(B * r, B * r + B)
        g.sync.dma_start(T.xs[:], T.x[:]).then_inc(S.loaded, 16)
        g.scalar.dma_start(T.land[:, mine], T.x[:, mine]).then_inc(S.own, 16)
        g.wait_ge(S.loaded, 16)

        feed = []
        for i, oc in enumerate(other_parity_chips(ch)):
            j = T.rank_of(oc * 8)
            feed.append(to(core + 2 + i // 2, engines(4 * i, 4), S.fed,
                           T.xs[:, B * j:B * j + 2 * B], T.relay[:, 2 * B * (i % 2):2 * B * (i % 2) + 2 * B]))
        g.remote_dma_fused(feed, local_sem=S.sent)

        sp = same_parity_chips(ch)
        first = []
        for i, dst in enumerate([sp[0] * 8, sp[0] * 8 + 4, sp[1] * 8, sp[1] * 8 + 4]):
            j = T.rank_of(dst)
            first.append(to(dst, engines(2 * i, 2), S.arrived, T.xs[:, B * j:B * j + B], T.land[:, mine]))
        sib = core ^ 4
        j = T.rank_of(sib)
        first.append(to(sib, engines(8, 8), S.arrived, T.xs[:, B * j:B * j + B], T.land[:, mine]))
        g.remote_dma_fused(first, local_sem=S.sent)
        second = []
        for i, dst in enumerate([sp[2] * 8, sp[2] * 8 + 4]):
            j = T.rank_of(dst)
            second.append(to(dst, engines(4 * i, 4), S.arrived, T.xs[:, B * j:B * j + B], T.land[:, mine]))
        g.remote_dma_fused(second, local_sem=S.sent)

        g.sync.wait_ge(S.arrived, 40)
        g.sync.wait_ge(S.own, 16)
        g.sync.dma_start(T.y[:], T.land[:]).then_inc(S.stored, 16)
        g.sync.wait_ge(S.stored, 16)
        g.wait_ge(S.sent, 16 + 16 + 8)

    elif k in (2, 3, 6, 7):
        h = k % 4 - 2
        owner = core - 2 - h
        r = T.rank_of(owner)
        g.wait_ge(S.fed, 8)
        fwd = []
        for i, oc in enumerate(other_parity_chips(ch)[2 * h:2 * h + 2]):
            for half in range(2):
                n = 2 * i + half
                fwd.append(to(oc * 8 + 4 * half, engines(2 * n, 2), S.arrived,
                              T.relay[:, B * n:B * n + B], T.land[:, B * r:B * r + B]))
        g.remote_dma_fused(fwd, local_sem=S.sent)
        g.wait_ge(S.sent, 8)
